import numpy as np
import ml_dtypes


def mxq(x, axis, fmt="e4m3"):
    dtype, down = {"e4m3": (ml_dtypes.float8_e4m3fn, 7), "e5m2": (ml_dtypes.float8_e5m2, 14)}[fmt]
    v = np.moveaxis(np.asarray(x, np.float32).astype(ml_dtypes.bfloat16).astype(np.float64), axis, -1)
    blocks = v.reshape(v.shape[:-1] + (-1, 32))
    amax = np.abs(blocks).max(-1, keepdims=True)
    byte = np.maximum(np.where(amax > 0, np.frexp(amax)[1] - 1 + 127, 0) - down, 1)
    scale = np.exp2(byte - 127.0)
    codes = (blocks / scale).astype(np.float32).astype(dtype).astype(np.float64)
    return np.moveaxis((codes * scale).reshape(v.shape), -1, axis)


WIDE = False


def mx_kscale(k):
    if not WIDE:
        return np.ones(k)
    levels = np.array([30, -30])
    if k % 512:
        return np.exp2(np.random.permutation(np.resize(levels, k // 32))).repeat(32)
    a = np.empty((k // 512, 16))
    for p in range(k // 512):
        a[p, :8] = np.random.permutation(np.resize(levels, 8))
        for g in range(8):
            far = levels[np.abs(levels - a[p, g]) >= 10]
            a[p, g + 8] = far[np.random.randint(len(far))]
    return np.exp2(a.ravel()).repeat(32)


def f64(x):
    return np.asarray(x).astype(np.float64)


def striped(idx):
    return np.tile(np.asarray(idx).reshape(-1, 16).T, (8, 1)).astype(np.uint16)


def unstriped(offs):
    return offs[:16].T.reshape(-1).astype(np.int64)


E2M1 = np.array([0.0, 0.5, 1.0, 1.5, 2.0, 3.0, 4.0, 6.0, -0.0, -0.5, -1.0, -1.5, -2.0, -3.0, -4.0, -6.0])


def pack_weight(w, fmt):
    k, n = w.shape
    w = f64(np.asarray(w, np.float32).astype(ml_dtypes.bfloat16)).reshape(k // 32, 32, n)
    amax = np.abs(w).max(1)
    if fmt in ("e4m3", "e5m2"):
        byte = np.frexp(amax)[1] - 1 + 127 - (7 if fmt == "e4m3" else 14)
    else:
        mant, ex = np.frexp(amax / 6.0)
        byte = np.where(mant > 0.5, ex, ex - 1) + 127
    byte = np.clip(np.where(amax > 0, byte, 1), 1, 254)
    scaled = (w * np.exp2(127.0 - byte)[:, None, :]).reshape(k, n).astype(np.float32)
    by_word = np.ascontiguousarray(scaled.reshape(k // 512, 128, 4, n).transpose(0, 1, 3, 2))
    if fmt in ("e4m3", "e5m2"):
        words = by_word.astype(ml_dtypes.float8_e4m3fn if fmt == "e4m3" else ml_dtypes.float8_e5m2).view(np.uint8)
    else:
        c = by_word.astype(ml_dtypes.float4_e2m1fn).view(np.uint8) & 0xF
        words = (c[..., 0::2] | (c[..., 1::2] << 4)).reshape(k // 512, 128, 2 * n)
    return np.ascontiguousarray(words), np.ascontiguousarray(byte.astype(np.uint8).reshape(k // 512, 16, n))


def unpack_weight(words, scales, fmt):
    g, _, n = scales.shape
    words = np.ascontiguousarray(words).reshape(g, 128, n, -1)
    if fmt in ("e4m3", "e5m2"):
        vals = words.view(ml_dtypes.float8_e4m3fn if fmt == "e4m3" else ml_dtypes.float8_e5m2).astype(np.float64)
    else:
        nib = np.empty((g, 128, n, 4), np.uint8)
        nib[..., 0::2] = words & 0xF
        nib[..., 1::2] = words >> 4
        vals = E2M1[nib]
    vals = vals * np.repeat(np.exp2(scales.astype(np.float64) - 127.0), 8, axis=1)[..., None]
    return vals.transpose(0, 1, 3, 2).reshape(g * 512, n)


K, T, J, R, F, Z, C, O, N, S = 512, 1024, 256, 512, 512, 1024, 512, 128, 256, 1024


def setup_inputs():
    n = np.random.standard_normal
    idx = np.random.permutation(T)[:J]
    idx2 = np.random.permutation(Z)[:J]
    idx3 = np.random.permutation(C)[:J]
    idx4 = np.random.permutation(C)[:O]
    idx5 = np.random.permutation(C)[:O]
    idx6 = np.random.permutation(J)[:O]
    idx7 = np.random.permutation(S)[:N]
    fk = mx_kscale(K)
    ff = mx_kscale(F)
    fr = mx_kscale(R)
    xtp = pack_weight(n((K, T)) / fk[:, None], "e4m3")
    xop = pack_weight(n((F, Z)) / ff[:, None], "e2m1")
    wp = pack_weight(n((K, R)) * 1 / np.sqrt(K) * fk[:, None] * fr, "e2m1")
    w0p = pack_weight(n((F, R)) * 1 / np.sqrt(F) * ff[:, None] * fr, "e5m2")
    w2p = pack_weight(n((F, R)) * 1 / np.sqrt(F) * ff[:, None], "e5m2")
    vsp = pack_weight(n((R, S)) * 1 / np.sqrt(R) / fr[:, None], "e5m2")
    return {
        "xt_words": xtp[0],
        "xt_scales": xtp[1],
        "xo_words": xop[0],
        "xo_scales": xop[1],
        "w_words": wp[0],
        "w_scales": wp[1],
        "w0_words": w0p[0],
        "w0_scales": w0p[1],
        "w2_words": w2p[0],
        "w2_scales": w2p[1],
        "vs_words": vsp[0],
        "vs_scales": vsp[1],
        "offs": striped(idx),
        "offs2": striped(idx2),
        "offs3": striped(idx3),
        "offs4": striped(idx4),
        "offs5": striped(idx5),
        "offs6": striped(idx6),
        "offs7": striped(idx7),
    }


def reference(xt_words, xt_scales, xo_words, xo_scales, w_words, w_scales, w0_words, w0_scales, w2_words, w2_scales, vs_words, vs_scales, offs, offs2, offs3, offs4, offs5, offs6, offs7):
    idx = unstriped(offs)
    idx2 = unstriped(offs2)
    idx3 = unstriped(offs3)
    idx4 = unstriped(offs4)
    idx5 = unstriped(offs5)
    idx6 = unstriped(offs6)
    idx7 = unstriped(offs7)
    xtu = unpack_weight(xt_words, xt_scales, "e4m3")
    xou = unpack_weight(xo_words, xo_scales, "e2m1")
    wu = unpack_weight(w_words, w_scales, "e2m1")
    w0u = unpack_weight(w0_words, w0_scales, "e5m2")
    w2u = unpack_weight(w2_words, w2_scales, "e5m2")
    vsu = unpack_weight(vs_words, vs_scales, "e5m2")
    xtidxg = xtu[:, idx]
    xoidx2g = xou[:, idx2]
    a = wu.T @ xtidxg + w0u.T @ xoidx2g
    b = w2u.T @ xoidx2g
    lb = b[:, 0:1]
    lb2 = b[:, 128:129]
    la = a[:, 0:1]
    pw = np.zeros((R, C))
    pw[:, idx3] = a
    hid = np.maximum(pw[:, idx4] * lb, pw[:, idx5] * lb2) - b[:, idx6] * la
    vsidx7g = vsu[:, idx7]
    hidq = mxq(hid, 0, "e4m3")
    y = vsidx7g.T @ hidq
    return y

@@ -1,0 +1,209 @@
+from contextlib import ExitStack
+
+import concourse.mybir as mybir
+
+F32 = mybir.dt.float32
+BF16 = mybir.dt.bfloat16
+I32 = mybir.dt.int32
+U32 = mybir.dt.uint32
+U16 = mybir.dt.uint16
+U8 = mybir.dt.uint8
+E4M3 = mybir.dt.float8_e4m3fn_x4
+E5M2 = mybir.dt.float8_e5m2_x4
+E2M1 = mybir.dt.float4_e2m1fn_x4
+COPY = mybir.ActivationFunctionType.Copy
+MAX = mybir.AluOpType.max
+SUB = mybir.AluOpType.subtract
+
+K, T, J, R, Z, C, O, N, S = 512, 1024, 256, 512, 1024, 512, 128, 256, 1024
+P = 128
+PACK = 4
+FLOPS = 2 * (3 * K * R * J + R * N * O)
+
+
+def tile_list_leadreads_noted_store_plain_kernel(
+    tc, xt_words, xt_scales, xo_words, xo_scales, w_words, w_scales, w0_words, w0_scales,
+    w2_words, w2_scales, vs_words, vs_scales, offs, offs2, offs3, offs4, offs5, offs6, offs7, out,
+):
+    nc = tc.nc
+    with ExitStack() as ctx:
+        sb = ctx.enter_context(tc.tile_pool(name="sb", bufs=1))
+        ps = ctx.enter_context(tc.psum_pool(name="ps", bufs=1))
+
+        def tile(shape, dtype, name):
+            return sb.tile(shape, dtype, name=name, align_bytes=64)
+
+        def load_list(src, name):
+            t = sb.tile(list(src.shape), U16, name=name)
+            nc.sync.dma_start(t[:], src)
+            return t
+
+        def load_words8(queue, src, name):
+            t = tile([P, src.shape[2]], U32, name)
+            queue.dma_start(t[:].bitcast(I32), src[0].rearrange("p n t -> p (n t)").bitcast(I32))
+            return t
+
+        def load_words4(queue, src, name):
+            t = tile([P, src.shape[2] // 2], U16, name)
+            queue.dma_start(t[:].bitcast(I32), src[0].bitcast(I32))
+            return t
+
+        def zeroed(shape, name):
+            t = tile(shape, U8, name)
+            nc.vector.memset(t[:].bitcast(I32), 0)
+            return t
+
+        def load_table_scales(queues, t, src):
+            for q in range(4):
+                queues[q].dma_start(t[32 * q : 32 * q + 4, :].bitcast(I32), src[0, 4 * q : 4 * q + 4, :].bitcast(I32))
+
+        def load_weight_scales(queues, t, src):
+            rows = src[0].bitcast(I32).rearrange("(h q r) n -> q r h n", h=2, q=2)
+            for q in range(2):
+                queues[q].dma_start(t[32 * q : 32 * q + 4, :].bitcast(I32).rearrange("p (h n) -> p h n", h=2), rows[q])
+
+        def gather(window, lst, dtype, name):
+            t = tile([P, J], dtype, name)
+            nc.vector.tensor_copy(t[:], window[:].indirect(lst[:]))
+            return t
+
+        def deal_words(src, dtype, name):
+            t = tile([P, R], dtype, name)
+            nc.scalar.copy(t[:].rearrange("p (t m) -> p m t", t=PACK), src[:].rearrange("p (m t) -> p m t", t=PACK))
+            return t
+
+        def deal_scales(stage, name):
+            nc.vector.tensor_copy(stage[64:128, 0:R].bitcast(I32), stage[0:64, R : 2 * R].bitcast(I32))
+            t = tile([P, R], U8, name)
+            nc.vector.tensor_copy(t[:].rearrange("p (t m) -> p m t", t=PACK), stage[:, 0:R].rearrange("p (m t) -> p m t", t=PACK))
+            return t
+
+        xo_st = zeroed([64, 2 * Z], "xo_st")
+        w0_st = zeroed([P, 2 * R], "w0_st")
+        w_st = zeroed([P, 2 * R], "w_st")
+        xt_s = zeroed([P, T], "xt_s")
+        vs_s = zeroed([P, S], "vs_s")
+        w2_pl = zeroed([P, R], "w2_pl")
+
+        l2 = load_list(offs2, "l2")
+        xo_w = load_words4(nc.scalar, xo_words, "xo_w")
+        w2_w = load_words8(nc.scalar, w2_words, "w2_w")
+        w0_w = load_words8(nc.scalar, w0_words, "w0_w")
+        xt_w = load_words8(nc.scalar, xt_words, "xt_w")
+        load_weight_scales((nc.sync, nc.sync), xo_st, xo_scales)
+        w2_st = tile([4, 4 * R], U8, "w2_st")
+        nc.sync.dma_start(w2_st[:].bitcast(I32).rearrange("r (q n) -> r q n", q=4), w2_scales[0].bitcast(I32).rearrange("(q r) n -> r q n", q=4))
+        load_weight_scales((nc.sync, nc.sync), w0_st, w0_scales)
+        load_weight_scales((nc.gpsimd, nc.gpsimd), w_st, w_scales)
+        l1 = load_list(offs, "l1")
+        w_w = load_words4(nc.sync, w_words, "w_w")
+        load_table_scales((nc.gpsimd, nc.sync, nc.sync, nc.sync), xt_s, xt_scales)
+        l3 = load_list(offs3, "l3")
+        l6 = load_list(offs6, "l6")
+        l4 = load_list(offs4, "l4")
+        l5 = load_list(offs5, "l5")
+        l7 = load_list(offs7, "l7")
+        vs_w = load_words8(nc.sync, vs_words, "vs_w")
+        load_table_scales((nc.gpsimd,) * 4, vs_s, vs_scales)
+
+        pw = []
+        for t in range(PACK):
+            page = tile([P, C], F32, "pw%d" % t)
+            nc.vector.memset(page[:], 0.0)
+            pw.append(page)
+
+        xo_s = tile([P, Z], U8, "xo_s")
+        for h in range(2):
+            nc.vector.tensor_copy(xo_s[64 * h : 64 * h + 64, :].bitcast(I32), xo_st[:, h * Z : (h + 1) * Z].bitcast(I32))
+        xo_gs = gather(xo_s, l2, U8, "xo_gs")
+        xo_gw = gather(xo_w, l2, U16, "xo_gw")
+        w2_d = deal_words(w2_w, U32, "w2_d")
+        for q in range(4):
+            nc.vector.tensor_copy(w2_pl[32 * q : 32 * q + 4, :].bitcast(I32), w2_st[:, q * R : (q + 1) * R].bitcast(I32))
+        w2_sd = tile([P, R], U8, "w2_sd")
+        nc.vector.tensor_copy(w2_sd[:].rearrange("p (t m) -> p m t", t=PACK), w2_pl[:].rearrange("p (m t) -> p m t", t=PACK))
+        w0_d = deal_words(w0_w, U32, "w0_d")
+        w0_sd = deal_scales(w0_st, "w0_sd")
+        w_d = deal_words(w_w, U16, "w_d")
+
+        b_ps = [ps.tile([P, 2, J], F32, name="b_ps%d" % h) for h in range(2)]
+        for t in range(PACK):
+            cols = slice(t * P, (t + 1) * P)
+            nc.tensor.matmul_mx(b_ps[t // 2][:, t % 2, :], lhsT=w2_d[:, cols].bitcast(E5M2), lhsT_scale=w2_sd[:, cols],
+                                rhs=xo_gw[:].bitcast(E2M1), rhs_scale=xo_gs[:], start=True, stop=True)
+
+        a_ps = [ps.tile([P, J], F32, name="a_ps%d" % t) for t in range(PACK)]
+        for t in range(PACK):
+            cols = slice(t * P, (t + 1) * P)
+            nc.tensor.matmul_mx(a_ps[t][:], lhsT=w0_d[:, cols].bitcast(E5M2), lhsT_scale=w0_sd[:, cols],
+                                rhs=xo_gw[:].bitcast(E2M1), rhs_scale=xo_gs[:], start=True, stop=False)
+
+        b = []
+        for t in range(PACK):
+            rows = tile([P, J], F32, "b%d" % t)
+            nc.scalar.activation(rows[:], b_ps[t // 2][:, t % 2, :], COPY)
+            b.append(rows)
+
+        w_sd = deal_scales(w_st, "w_sd")
+        xt_gw = gather(xt_w, l1, U32, "xt_gw")
+        xt_gs = gather(xt_s, l1, U8, "xt_gs")
+        for t in range(PACK):
+            cols = slice(t * P, (t + 1) * P)
+            nc.tensor.matmul_mx(a_ps[t][:], lhsT=w_d[:, cols].bitcast(E2M1), lhsT_scale=w_sd[:, cols],
+                                rhs=xt_gw[:].bitcast(E4M3), rhs_scale=xt_gs[:], start=False, stop=True)
+
+        a = []
+        for t in range(PACK):
+            rows = tile([P, J], F32, "a%d" % t)
+            if t == 0:
+                nc.vector.tensor_copy(rows[:], a_ps[t][:])
+            else:
+                nc.scalar.copy(rows[:], a_ps[t][:])
+            a.append(rows)
+
+        g4 = tile([P, PACK, O], F32, "g4")
+        g5 = tile([P, PACK, O], F32, "g5")
+        g6 = tile([P, PACK, O], F32, "g6")
+        top = tile([P, PACK, O], F32, "top")
+
+        def scatter(t):
+            if t == 1:
+                nc.scalar.activation(pw[t][:].indirect(l3[:]), a[t][:], COPY)
+            else:
+                nc.vector.tensor_copy(pw[t][:].indirect(l3[:]), a[t][:])
+
+        def look_board(t):
+            nc.scalar.activation(g4[:, t, :], pw[t][:].indirect(l4[:]), COPY, scale=b[t][:, 0:1])
+            nc.scalar.activation(g5[:, t, :], pw[t][:].indirect(l5[:]), COPY, scale=b[t][:, 128:129])
+
+        def look_b(t):
+            nc.scalar.activation(g6[:, t, :], b[t][:].indirect(l6[:]), COPY, scale=a[t][:, 0:1])
+
+        for t in range(PACK):
+            scatter(t)
+        vs_gs = gather(vs_s, l7, U8, "vs_gs")
+        vs_gw = gather(vs_w, l7, U32, "vs_gw")
+        for t in range(PACK):
+            look_b(t)
+        for t in range(PACK):
+            look_board(t)
+            nc.vector.tensor_tensor(top[:, t, :], g4[:, t, :], g5[:, t, :], MAX)
+
+        hid_b = tile([P, O, PACK], BF16, "hid_b")
+        nc.vector.tensor_tensor(hid_b[:].rearrange("p (c i) t -> p c t i", i=4), top[:].rearrange("p t (c i) -> p c t i", i=4),
+                                g6[:].rearrange("p t (c i) -> p c t i", i=4), SUB)
+        hid_w = tile([P, O], U32, "hid_w")
+        hid_s = tile([P, O], U8, "hid_s")
+        nc.vector.quantize_mx(out=hid_w[:].bitcast(E4M3), scales=hid_s[:], in_=hid_b[:].rearrange("p o t -> p (o t)"))
+
+        y = tile([P, 2, O], F32, "y")
+        for h in range(2):
+            cols = slice(h * P, (h + 1) * P)
+            y_ps = ps.tile([P, O], F32, name="y_ps%d" % h)
+            nc.tensor.matmul_mx(y_ps[:], lhsT=vs_gw[:, cols].bitcast(E5M2), lhsT_scale=vs_gs[:, cols],
+                                rhs=hid_w[:].bitcast(E4M3), rhs_scale=hid_s[:], start=True, stop=True)
+            if h == 0:
+                nc.vector.tensor_copy(y[:, h, :], y_ps[:])
+            else:
+                nc.scalar.copy(y[:, h, :], y_ps[:])
+        nc.sync.dma_start(out.rearrange("(h p) o -> p h o", h=2), y[:])

@@ -30,8 +30,8 @@ def tile_list_leadreads_noted_store_plain_kernel(
         sb = ctx.enter_context(tc.tile_pool(name="sb", bufs=1))
         ps = ctx.enter_context(tc.psum_pool(name="ps", bufs=1))
 
-        def tile(shape, dtype, name):
-            return sb.tile(shape, dtype, name=name, align_bytes=64)
+        def tile(shape, dtype, name, tag=""):
+            return sb.tile(shape, dtype, name=name, tag=tag, align_bytes=64)
 
         def load_list(src, name):
             t = sb.tile(list(src.shape), U16, name=name)
@@ -48,8 +48,8 @@ def tile_list_leadreads_noted_store_plain_kernel(
             queue.dma_start(t[:].bitcast(I32), src[0].bitcast(I32))
             return t
 
-        def zeroed(shape, name):
-            t = tile(shape, U8, name)
+        def zeroed(shape, name, tag=""):
+            t = tile(shape, U8, name, tag)
             nc.vector.memset(t[:].bitcast(I32), 0)
             return t
 
@@ -57,54 +57,57 @@ def tile_list_leadreads_noted_store_plain_kernel(
             for q in range(4):
                 queues[q].dma_start(t[32 * q : 32 * q + 4, :].bitcast(I32), src[0, 4 * q : 4 * q + 4, :].bitcast(I32))
 
-        def load_weight_scales(queues, t, src):
+        def load_weight_scales(t, src, half):
             rows = src[0].bitcast(I32).rearrange("(h q r) n -> q r h n", h=2, q=2)
             for q in range(2):
-                queues[q].dma_start(t[32 * q : 32 * q + 4, :].bitcast(I32).rearrange("p (h n) -> p h n", h=2), rows[q])
+                p0 = 64 * half + 32 * q
+                nc.sync.dma_start(t[p0 : p0 + 4, :].bitcast(I32).rearrange("p (h n) -> p h n", h=2), rows[q])
 
         def gather(window, lst, dtype, name):
             t = tile([P, J], dtype, name)
             nc.vector.tensor_copy(t[:], window[:].indirect(lst[:]))
             return t
 
-        def deal_words(src, dtype, name):
+        def deal_words(src, dtype, name, walk="p m t"):
             t = tile([P, R], dtype, name)
-            nc.scalar.copy(t[:].rearrange("p (t m) -> p m t", t=PACK), src[:].rearrange("p (m t) -> p m t", t=PACK))
+            nc.scalar.copy(t[:].rearrange("p (t m) -> " + walk, t=PACK), src[:].rearrange("p (m t) -> " + walk, t=PACK))
             return t
 
-        def deal_scales(stage, name):
-            nc.vector.tensor_copy(stage[64:128, 0:R].bitcast(I32), stage[0:64, R : 2 * R].bitcast(I32))
+        def deal_scales(stage, name, half):
+            other = 1 - half
+            plane = slice(half * R, (half + 1) * R)
+            nc.vector.tensor_copy(stage[64 * other : 64 * other + 64, plane].bitcast(I32),
+                                  stage[64 * half : 64 * half + 64, other * R : (other + 1) * R].bitcast(I32))
             t = tile([P, R], U8, name)
-            nc.vector.tensor_copy(t[:].rearrange("p (t m) -> p m t", t=PACK), stage[:, 0:R].rearrange("p (m t) -> p m t", t=PACK))
+            nc.vector.tensor_copy(t[:].rearrange("p (t m) -> p t m", t=PACK), stage[:, plane].rearrange("p (m t) -> p t m", t=PACK))
             return t
 
-        xo_st = zeroed([64, 2 * Z], "xo_st")
+        xo_s = zeroed([P, Z], "xo_s")
+        w2_st = zeroed([P, 2 * R], "w2_st")
         w0_st = zeroed([P, 2 * R], "w0_st")
         w_st = zeroed([P, 2 * R], "w_st")
         xt_s = zeroed([P, T], "xt_s")
-        vs_s = zeroed([P, S], "vs_s")
-        w2_pl = zeroed([P, R], "w2_pl")
+        vs_s = zeroed([P, S], "vs_s", "vs_s_then_top")
 
         l2 = load_list(offs2, "l2")
         xo_w = load_words4(nc.scalar, xo_words, "xo_w")
-        w2_w = load_words8(nc.scalar, w2_words, "w2_w")
+        load_table_scales((nc.sync, nc.scalar, nc.sync, nc.scalar), xo_s, xo_scales)
+        w2_w = load_words8(nc.sync, w2_words, "w2_w")
         w0_w = load_words8(nc.scalar, w0_words, "w0_w")
-        xt_w = load_words8(nc.scalar, xt_words, "xt_w")
-        load_weight_scales((nc.sync, nc.sync), xo_st, xo_scales)
-        w2_st = tile([4, 4 * R], U8, "w2_st")
-        nc.sync.dma_start(w2_st[:].bitcast(I32).rearrange("r (q n) -> r q n", q=4), w2_scales[0].bitcast(I32).rearrange("(q r) n -> r q n", q=4))
-        load_weight_scales((nc.sync, nc.sync), w0_st, w0_scales)
-        load_weight_scales((nc.gpsimd, nc.gpsimd), w_st, w_scales)
+        load_weight_scales(w2_st, w2_scales, 0)
+        load_weight_scales(w0_st, w0_scales, 1)
         l1 = load_list(offs, "l1")
+        xt_w = load_words8(nc.sync, xt_words, "xt_w")
         w_w = load_words4(nc.sync, w_words, "w_w")
-        load_table_scales((nc.gpsimd, nc.sync, nc.sync, nc.sync), xt_s, xt_scales)
+        load_weight_scales(w_st, w_scales, 0)
+        load_table_scales((nc.sync,) * 4, xt_s, xt_scales)
         l3 = load_list(offs3, "l3")
         l6 = load_list(offs6, "l6")
         l4 = load_list(offs4, "l4")
         l5 = load_list(offs5, "l5")
         l7 = load_list(offs7, "l7")
         vs_w = load_words8(nc.sync, vs_words, "vs_w")
-        load_table_scales((nc.gpsimd,) * 4, vs_s, vs_scales)
+        load_table_scales((nc.sync,) * 4, vs_s, vs_scales)
 
         pw = []
         for t in range(PACK):
@@ -112,19 +115,13 @@ def tile_list_leadreads_noted_store_plain_kernel(
             nc.vector.memset(page[:], 0.0)
             pw.append(page)
 
-        xo_s = tile([P, Z], U8, "xo_s")
-        for h in range(2):
-            nc.vector.tensor_copy(xo_s[64 * h : 64 * h + 64, :].bitcast(I32), xo_st[:, h * Z : (h + 1) * Z].bitcast(I32))
-        xo_gs = gather(xo_s, l2, U8, "xo_gs")
         xo_gw = gather(xo_w, l2, U16, "xo_gw")
+        xo_gs = gather(xo_s, l2, U8, "xo_gs")
         w2_d = deal_words(w2_w, U32, "w2_d")
-        for q in range(4):
-            nc.vector.tensor_copy(w2_pl[32 * q : 32 * q + 4, :].bitcast(I32), w2_st[:, q * R : (q + 1) * R].bitcast(I32))
-        w2_sd = tile([P, R], U8, "w2_sd")
-        nc.vector.tensor_copy(w2_sd[:].rearrange("p (t m) -> p m t", t=PACK), w2_pl[:].rearrange("p (m t) -> p m t", t=PACK))
+        w2_sd = deal_scales(w2_st, "w2_sd", 0)
         w0_d = deal_words(w0_w, U32, "w0_d")
-        w0_sd = deal_scales(w0_st, "w0_sd")
-        w_d = deal_words(w_w, U16, "w_d")
+        w0_sd = deal_scales(w0_st, "w0_sd", 1)
+        w_d = deal_words(w_w, U16, "w_d", "p t m")
 
         b_ps = [ps.tile([P, 2, J], F32, name="b_ps%d" % h) for h in range(2)]
         for t in range(PACK):
@@ -144,8 +141,8 @@ def tile_list_leadreads_noted_store_plain_kernel(
             nc.scalar.activation(rows[:], b_ps[t // 2][:, t % 2, :], COPY)
             b.append(rows)
 
-        w_sd = deal_scales(w_st, "w_sd")
         xt_gw = gather(xt_w, l1, U32, "xt_gw")
+        w_sd = deal_scales(w_st, "w_sd", 0)
         xt_gs = gather(xt_s, l1, U8, "xt_gs")
         for t in range(PACK):
             cols = slice(t * P, (t + 1) * P)
@@ -164,13 +161,12 @@ def tile_list_leadreads_noted_store_plain_kernel(
         g4 = tile([P, PACK, O], F32, "g4")
         g5 = tile([P, PACK, O], F32, "g5")
         g6 = tile([P, PACK, O], F32, "g6")
-        top = tile([P, PACK, O], F32, "top")
 
-        def scatter(t):
-            if t == 1:
-                nc.scalar.activation(pw[t][:].indirect(l3[:]), a[t][:], COPY)
-            else:
-                nc.vector.tensor_copy(pw[t][:].indirect(l3[:]), a[t][:])
+        def scatter_s(t, lo, hi):
+            nc.scalar.activation(pw[t][:].indirect(l3[:, lo // 16 : hi // 16]), a[t][:, lo:hi], COPY)
+
+        def scatter_v(t, lo, hi):
+            nc.vector.tensor_copy(pw[t][:].indirect(l3[:, lo // 16 : hi // 16]), a[t][:, lo:hi])
 
         def look_board(t):
             nc.scalar.activation(g4[:, t, :], pw[t][:].indirect(l4[:]), COPY, scale=b[t][:, 0:1])
@@ -179,10 +175,14 @@ def tile_list_leadreads_noted_store_plain_kernel(
         def look_b(t):
             nc.scalar.activation(g6[:, t, :], b[t][:].indirect(l6[:]), COPY, scale=a[t][:, 0:1])
 
-        for t in range(PACK):
-            scatter(t)
-        vs_gs = gather(vs_s, l7, U8, "vs_gs")
+        scatter_v(0, 0, J)
+        scatter_s(1, 0, J)
+        scatter_s(3, 0, 64)
+        scatter_v(2, 0, J)
+        scatter_v(3, 64, J)
         vs_gw = gather(vs_w, l7, U32, "vs_gw")
+        vs_gs = gather(vs_s, l7, U8, "vs_gs")
+        top = tile([P, PACK, O], F32, "top", "vs_s_then_top")
         for t in range(PACK):
             look_b(t)
         for t in range(PACK):
@@ -204,6 +204,7 @@ def tile_list_leadreads_noted_store_plain_kernel(
                                 rhs=hid_w[:].bitcast(E4M3), rhs_scale=hid_s[:], start=True, stop=True)
             if h == 0:
                 nc.vector.tensor_copy(y[:, h, :], y_ps[:])
+                nc.sync.dma_start(out[cols, :], y[:, h, :])
             else:
                 nc.scalar.copy(y[:, h, :], y_ps[:])
-        nc.sync.dma_start(out.rearrange("(h p) o -> p h o", h=2), y[:])
+                nc.scalar.dma_start(out[cols, :], y[:, h, :])

@@ -18,6 +18,11 @@ SUB = mybir.AluOpType.subtract
 K, T, J, R, Z, C, O, N, S = 512, 1024, 256, 512, 1024, 512, 128, 256, 1024
 P = 128
 PACK = 4
+QUAD = 32
+HALF = 64
+PER_COLUMN = 16
+LB2_SLOT = 128
+SCALAR_SHARE = 64
 FLOPS = 2 * (3 * K * R * J + R * N * O)
 
 
@@ -34,71 +39,72 @@ def tile_list_leadreads_noted_store_plain_kernel(
             return sb.tile(shape, dtype, name=name, tag=tag, align_bytes=64)
 
         def load_list(src, name):
-            t = sb.tile(list(src.shape), U16, name=name)
-            nc.sync.dma_start(t[:], src)
-            return t
+            lst = sb.tile(list(src.shape), U16, name=name)
+            nc.sync.dma_start(lst[:], src)
+            return lst
 
-        def load_words8(queue, src, name):
-            t = tile([P, src.shape[2]], U32, name)
-            queue.dma_start(t[:].bitcast(I32), src[0].rearrange("p n t -> p (n t)").bitcast(I32))
-            return t
+        def load_fp8_words(queue, src, name):
+            words = tile([P, src.shape[2]], U32, name)
+            queue.dma_start(words[:].bitcast(I32), src[0].rearrange("p n t -> p (n t)").bitcast(I32))
+            return words
 
-        def load_words4(queue, src, name):
-            t = tile([P, src.shape[2] // 2], U16, name)
-            queue.dma_start(t[:].bitcast(I32), src[0].bitcast(I32))
-            return t
+        def load_fp4_words(queue, src, name):
+            words = tile([P, src.shape[2] // 2], U16, name)
+            queue.dma_start(words[:].bitcast(I32), src[0].bitcast(I32))
+            return words
 
-        def zeroed(shape, name, tag=""):
-            t = tile(shape, U8, name, tag)
-            nc.vector.memset(t[:].bitcast(I32), 0)
-            return t
+        def zeroed_bytes(columns, name, tag=""):
+            rows = tile([P, columns], U8, name, tag)
+            nc.vector.memset(rows[:].bitcast(I32), 0)
+            return rows
 
-        def load_table_scales(queues, t, src):
+        def load_table_scales(queues, plane, src):
             for q in range(4):
-                queues[q].dma_start(t[32 * q : 32 * q + 4, :].bitcast(I32), src[0, 4 * q : 4 * q + 4, :].bitcast(I32))
+                queues[q].dma_start(plane[QUAD * q : QUAD * q + 4, :].bitcast(I32), src[0, 4 * q : 4 * q + 4, :].bitcast(I32))
 
-        def load_weight_scales(t, src, half):
-            rows = src[0].bitcast(I32).rearrange("(h q r) n -> q r h n", h=2, q=2)
+        def load_weight_scales(stage, src, half):
+            rows = src[0].bitcast(I32).rearrange("(h q i) n -> q i h n", h=2, q=2)
             for q in range(2):
-                p0 = 64 * half + 32 * q
-                nc.sync.dma_start(t[p0 : p0 + 4, :].bitcast(I32).rearrange("p (h n) -> p h n", h=2), rows[q])
+                first = HALF * half + QUAD * q
+                nc.sync.dma_start(stage[first : first + 4, :].bitcast(I32).rearrange("i (h n) -> i h n", h=2), rows[q])
 
         def gather(window, lst, dtype, name):
-            t = tile([P, J], dtype, name)
-            nc.vector.tensor_copy(t[:], window[:].indirect(lst[:]))
-            return t
+            picked = tile([P, J], dtype, name)
+            nc.vector.tensor_copy(picked[:], window[:].indirect(lst[:]))
+            return picked
 
-        def deal_words(src, dtype, name, walk="p m t"):
-            t = tile([P, R], dtype, name)
-            nc.scalar.copy(t[:].rearrange("p (t m) -> " + walk, t=PACK), src[:].rearrange("p (m t) -> " + walk, t=PACK))
-            return t
+        def deal_words(words, dtype, name, walk):
+            dealt = tile([P, R], dtype, name)
+            nc.scalar.copy(dealt[:].rearrange("p (t m) -> " + walk, t=PACK), words[:].rearrange("p (m t) -> " + walk, t=PACK))
+            return dealt
 
         def deal_scales(stage, name, half):
             other = 1 - half
             plane = slice(half * R, (half + 1) * R)
-            nc.vector.tensor_copy(stage[64 * other : 64 * other + 64, plane].bitcast(I32),
-                                  stage[64 * half : 64 * half + 64, other * R : (other + 1) * R].bitcast(I32))
-            t = tile([P, R], U8, name)
-            nc.vector.tensor_copy(t[:].rearrange("p (t m) -> p t m", t=PACK), stage[:, plane].rearrange("p (m t) -> p t m", t=PACK))
-            return t
+            nc.vector.tensor_copy(stage[HALF * other : HALF * (other + 1), plane].bitcast(I32),
+                                  stage[HALF * half : HALF * (half + 1), other * R : (other + 1) * R].bitcast(I32))
+            dealt = tile([P, R], U8, name)
+            nc.vector.tensor_copy(dealt[:].rearrange("p (t m) -> p t m", t=PACK), stage[:, plane].rearrange("p (m t) -> p t m", t=PACK))
+            return dealt
 
-        xo_s = zeroed([P, Z], "xo_s")
-        w2_st = zeroed([P, 2 * R], "w2_st")
-        w0_st = zeroed([P, 2 * R], "w0_st")
-        w_st = zeroed([P, 2 * R], "w_st")
-        xt_s = zeroed([P, T], "xt_s")
-        vs_s = zeroed([P, S], "vs_s", "vs_s_then_top")
+        shared_tag = "vs_s_then_top"
+        xo_s = zeroed_bytes(Z, "xo_s")
+        w2_st = zeroed_bytes(2 * R, "w2_st")
+        w0_st = zeroed_bytes(2 * R, "w0_st")
+        w_st = zeroed_bytes(2 * R, "w_st")
+        xt_s = zeroed_bytes(T, "xt_s")
+        vs_s = zeroed_bytes(S, "vs_s", shared_tag)
 
         l2 = load_list(offs2, "l2")
-        xo_w = load_words4(nc.scalar, xo_words, "xo_w")
+        xo_w = load_fp4_words(nc.scalar, xo_words, "xo_w")
         load_table_scales((nc.sync, nc.scalar, nc.sync, nc.scalar), xo_s, xo_scales)
-        w2_w = load_words8(nc.sync, w2_words, "w2_w")
-        w0_w = load_words8(nc.scalar, w0_words, "w0_w")
+        w2_w = load_fp8_words(nc.sync, w2_words, "w2_w")
+        w0_w = load_fp8_words(nc.scalar, w0_words, "w0_w")
         load_weight_scales(w2_st, w2_scales, 0)
         load_weight_scales(w0_st, w0_scales, 1)
         l1 = load_list(offs, "l1")
-        xt_w = load_words8(nc.sync, xt_words, "xt_w")
-        w_w = load_words4(nc.sync, w_words, "w_w")
+        xt_w = load_fp8_words(nc.sync, xt_words, "xt_w")
+        w_w = load_fp4_words(nc.sync, w_words, "w_w")
         load_weight_scales(w_st, w_scales, 0)
         load_table_scales((nc.sync,) * 4, xt_s, xt_scales)
         l3 = load_list(offs3, "l3")
@@ -106,7 +112,7 @@ def tile_list_leadreads_noted_store_plain_kernel(
         l4 = load_list(offs4, "l4")
         l5 = load_list(offs5, "l5")
         l7 = load_list(offs7, "l7")
-        vs_w = load_words8(nc.sync, vs_words, "vs_w")
+        vs_w = load_fp8_words(nc.sync, vs_words, "vs_w")
         load_table_scales((nc.sync,) * 4, vs_s, vs_scales)
 
         pw = []
@@ -117,13 +123,13 @@ def tile_list_leadreads_noted_store_plain_kernel(
 
         xo_gw = gather(xo_w, l2, U16, "xo_gw")
         xo_gs = gather(xo_s, l2, U8, "xo_gs")
-        w2_d = deal_words(w2_w, U32, "w2_d")
+        w2_d = deal_words(w2_w, U32, "w2_d", "p m t")
         w2_sd = deal_scales(w2_st, "w2_sd", 0)
-        w0_d = deal_words(w0_w, U32, "w0_d")
+        w0_d = deal_words(w0_w, U32, "w0_d", "p m t")
         w0_sd = deal_scales(w0_st, "w0_sd", 1)
         w_d = deal_words(w_w, U16, "w_d", "p t m")
 
-        b_ps = [ps.tile([P, 2, J], F32, name="b_ps%d" % h) for h in range(2)]
+        b_ps = [ps.tile([P, 2, J], F32, name="b_ps%d" % bank) for bank in range(2)]
         for t in range(PACK):
             cols = slice(t * P, (t + 1) * P)
             nc.tensor.matmul_mx(b_ps[t // 2][:, t % 2, :], lhsT=w2_d[:, cols].bitcast(E5M2), lhsT_scale=w2_sd[:, cols],
@@ -149,62 +155,53 @@ def tile_list_leadreads_noted_store_plain_kernel(
             nc.tensor.matmul_mx(a_ps[t][:], lhsT=w_d[:, cols].bitcast(E2M1), lhsT_scale=w_sd[:, cols],
                                 rhs=xt_gw[:].bitcast(E4M3), rhs_scale=xt_gs[:], start=False, stop=True)
 
-        a = []
-        for t in range(PACK):
+        a = [tile([P, J], F32, "a0")]
+        nc.vector.tensor_copy(a[0][:], a_ps[0][:])
+        for t in range(1, PACK):
             rows = tile([P, J], F32, "a%d" % t)
-            if t == 0:
-                nc.vector.tensor_copy(rows[:], a_ps[t][:])
-            else:
-                nc.scalar.copy(rows[:], a_ps[t][:])
+            nc.scalar.copy(rows[:], a_ps[t][:])
             a.append(rows)
 
-        g4 = tile([P, PACK, O], F32, "g4")
-        g5 = tile([P, PACK, O], F32, "g5")
-        g6 = tile([P, PACK, O], F32, "g6")
+        look4 = tile([P, PACK, O], F32, "look4")
+        look5 = tile([P, PACK, O], F32, "look5")
+        look6 = tile([P, PACK, O], F32, "look6")
 
-        def scatter_s(t, lo, hi):
-            nc.scalar.activation(pw[t][:].indirect(l3[:, lo // 16 : hi // 16]), a[t][:, lo:hi], COPY)
-
-        def scatter_v(t, lo, hi):
-            nc.vector.tensor_copy(pw[t][:].indirect(l3[:, lo // 16 : hi // 16]), a[t][:, lo:hi])
-
-        def look_board(t):
-            nc.scalar.activation(g4[:, t, :], pw[t][:].indirect(l4[:]), COPY, scale=b[t][:, 0:1])
-            nc.scalar.activation(g5[:, t, :], pw[t][:].indirect(l5[:]), COPY, scale=b[t][:, 128:129])
+        def board_at(t, lo, hi):
+            return pw[t][:].indirect(l3[:, lo // PER_COLUMN : hi // PER_COLUMN])
 
         def look_b(t):
-            nc.scalar.activation(g6[:, t, :], b[t][:].indirect(l6[:]), COPY, scale=a[t][:, 0:1])
+            nc.scalar.activation(look6[:, t, :], b[t][:].indirect(l6[:]), COPY, scale=a[t][:, 0:1])
 
-        scatter_v(0, 0, J)
-        scatter_s(1, 0, J)
-        scatter_s(3, 0, 64)
-        scatter_v(2, 0, J)
-        scatter_v(3, 64, J)
+        nc.vector.tensor_copy(board_at(0, 0, J), a[0][:])
+        nc.scalar.activation(board_at(1, 0, J), a[1][:], COPY)
+        nc.scalar.activation(board_at(3, 0, SCALAR_SHARE), a[3][:, 0:SCALAR_SHARE], COPY)
+        nc.vector.tensor_copy(board_at(2, 0, J), a[2][:])
+        nc.vector.tensor_copy(board_at(3, SCALAR_SHARE, J), a[3][:, SCALAR_SHARE:J])
         vs_gw = gather(vs_w, l7, U32, "vs_gw")
         vs_gs = gather(vs_s, l7, U8, "vs_gs")
-        top = tile([P, PACK, O], F32, "top", "vs_s_then_top")
-        for t in range(PACK):
+        top = tile([P, PACK, O], F32, "top", shared_tag)
+
+        for t in range(PACK // 2):
             look_b(t)
         for t in range(PACK):
-            look_board(t)
-            nc.vector.tensor_tensor(top[:, t, :], g4[:, t, :], g5[:, t, :], MAX)
+            nc.scalar.activation(look4[:, t, :], pw[t][:].indirect(l4[:]), COPY, scale=b[t][:, 0:1])
+            nc.scalar.activation(look5[:, t, :], pw[t][:].indirect(l5[:]), COPY, scale=b[t][:, LB2_SLOT : LB2_SLOT + 1])
+            nc.vector.tensor_tensor(top[:, t, :], look4[:, t, :], look5[:, t, :], MAX)
+        for t in range(PACK // 2, PACK):
+            look_b(t)
 
         hid_b = tile([P, O, PACK], BF16, "hid_b")
         nc.vector.tensor_tensor(hid_b[:].rearrange("p (c i) t -> p c t i", i=4), top[:].rearrange("p t (c i) -> p c t i", i=4),
-                                g6[:].rearrange("p t (c i) -> p c t i", i=4), SUB)
+                                look6[:].rearrange("p t (c i) -> p c t i", i=4), SUB)
         hid_w = tile([P, O], U32, "hid_w")
         hid_s = tile([P, O], U8, "hid_s")
         nc.vector.quantize_mx(out=hid_w[:].bitcast(E4M3), scales=hid_s[:], in_=hid_b[:].rearrange("p o t -> p (o t)"))
 
         y = tile([P, 2, O], F32, "y")
-        for h in range(2):
+        for h, (copy_out, queue) in enumerate(((nc.vector.tensor_copy, nc.sync), (nc.scalar.copy, nc.scalar))):
             cols = slice(h * P, (h + 1) * P)
             y_ps = ps.tile([P, O], F32, name="y_ps%d" % h)
             nc.tensor.matmul_mx(y_ps[:], lhsT=vs_gw[:, cols].bitcast(E5M2), lhsT_scale=vs_gs[:, cols],
                                 rhs=hid_w[:].bitcast(E4M3), rhs_scale=hid_s[:], start=True, stop=True)
-            if h == 0:
-                nc.vector.tensor_copy(y[:, h, :], y_ps[:])
-                nc.sync.dma_start(out[cols, :], y[:, h, :])
-            else:
-                nc.scalar.copy(y[:, h, :], y_ps[:])
-                nc.scalar.dma_start(out[cols, :], y[:, h, :])
+            copy_out(y[:, h, :], y_ps[:])
+            queue.dma_start(out[cols, :], y[:, h, :])

from contextlib import ExitStack

import concourse.mybir as mybir

F32 = mybir.dt.float32
BF16 = mybir.dt.bfloat16
I32 = mybir.dt.int32
U32 = mybir.dt.uint32
U16 = mybir.dt.uint16
U8 = mybir.dt.uint8
E4M3 = mybir.dt.float8_e4m3fn_x4
E5M2 = mybir.dt.float8_e5m2_x4
E2M1 = mybir.dt.float4_e2m1fn_x4
COPY = mybir.ActivationFunctionType.Copy
MAX = mybir.AluOpType.max
SUB = mybir.AluOpType.subtract

K, T, J, R, Z, C, O, N, S = 512, 1024, 256, 512, 1024, 512, 128, 256, 1024
P = 128
PACK = 4
QUAD = 32
HALF = 64
PER_COLUMN = 16
LB2_SLOT = 128
SCALAR_SHARE = 64
FLOPS = 2 * (3 * K * R * J + R * N * O)


def tile_list_leadreads_noted_store_plain_kernel(
    tc, xt_words, xt_scales, xo_words, xo_scales, w_words, w_scales, w0_words, w0_scales,
    w2_words, w2_scales, vs_words, vs_scales, offs, offs2, offs3, offs4, offs5, offs6, offs7, out,
):
    nc = tc.nc
    with ExitStack() as ctx:
        sb = ctx.enter_context(tc.tile_pool(name="sb", bufs=1))
        ps = ctx.enter_context(tc.psum_pool(name="ps", bufs=1))

        def tile(shape, dtype, name, tag=""):
            return sb.tile(shape, dtype, name=name, tag=tag, align_bytes=64)

        def load_list(src, name):
            lst = sb.tile(list(src.shape), U16, name=name)
            nc.sync.dma_start(lst[:], src)
            return lst

        def load_fp8_words(queue, src, name):
            words = tile([P, src.shape[2]], U32, name)
            queue.dma_start(words[:].bitcast(I32), src[0].rearrange("p n t -> p (n t)").bitcast(I32))
            return words

        def load_fp4_words(queue, src, name):
            words = tile([P, src.shape[2] // 2], U16, name)
            queue.dma_start(words[:].bitcast(I32), src[0].bitcast(I32))
            return words

        def zeroed_bytes(columns, name, tag=""):
            rows = tile([P, columns], U8, name, tag)
            nc.vector.memset(rows[:].bitcast(I32), 0)
            return rows

        def load_table_scales(queues, plane, src):
            for q in range(4):
                queues[q].dma_start(plane[QUAD * q : QUAD * q + 4, :].bitcast(I32), src[0, 4 * q : 4 * q + 4, :].bitcast(I32))

        def load_weight_scales(stage, src, half):
            rows = src[0].bitcast(I32).rearrange("(h q i) n -> q i h n", h=2, q=2)
            for q in range(2):
                first = HALF * half + QUAD * q
                nc.sync.dma_start(stage[first : first + 4, :].bitcast(I32).rearrange("i (h n) -> i h n", h=2), rows[q])

        def gather(window, lst, dtype, name):
            picked = tile([P, J], dtype, name)
            nc.vector.tensor_copy(picked[:], window[:].indirect(lst[:]))
            return picked

        def deal_words(words, dtype, name, walk):
            dealt = tile([P, R], dtype, name)
            nc.scalar.copy(dealt[:].rearrange("p (t m) -> " + walk, t=PACK), words[:].rearrange("p (m t) -> " + walk, t=PACK))
            return dealt

        def deal_scales(stage, name, half):
            other = 1 - half
            plane = slice(half * R, (half + 1) * R)
            nc.vector.tensor_copy(stage[HALF * other : HALF * (other + 1), plane].bitcast(I32),
                                  stage[HALF * half : HALF * (half + 1), other * R : (other + 1) * R].bitcast(I32))
            dealt = tile([P, R], U8, name)
            nc.vector.tensor_copy(dealt[:].rearrange("p (t m) -> p t m", t=PACK), stage[:, plane].rearrange("p (m t) -> p t m", t=PACK))
            return dealt

        shared_tag = "vs_s_then_top"
        xo_s = zeroed_bytes(Z, "xo_s")
        w2_st = zeroed_bytes(2 * R, "w2_st")
        w0_st = zeroed_bytes(2 * R, "w0_st")
        w_st = zeroed_bytes(2 * R, "w_st")
        xt_s = zeroed_bytes(T, "xt_s")
        vs_s = zeroed_bytes(S, "vs_s", shared_tag)

        l2 = load_list(offs2, "l2")
        xo_w = load_fp4_words(nc.scalar, xo_words, "xo_w")
        load_table_scales((nc.sync, nc.scalar, nc.sync, nc.scalar), xo_s, xo_scales)
        w2_w = load_fp8_words(nc.sync, w2_words, "w2_w")
        w0_w = load_fp8_words(nc.scalar, w0_words, "w0_w")
        load_weight_scales(w2_st, w2_scales, 0)
        load_weight_scales(w0_st, w0_scales, 1)
        l1 = load_list(offs, "l1")
        xt_w = load_fp8_words(nc.sync, xt_words, "xt_w")
        w_w = load_fp4_words(nc.sync, w_words, "w_w")
        load_weight_scales(w_st, w_scales, 0)
        load_table_scales((nc.sync,) * 4, xt_s, xt_scales)
        l3 = load_list(offs3, "l3")
        l6 = load_list(offs6, "l6")
        l4 = load_list(offs4, "l4")
        l5 = load_list(offs5, "l5")
        l7 = load_list(offs7, "l7")
        vs_w = load_fp8_words(nc.sync, vs_words, "vs_w")
        load_table_scales((nc.sync,) * 4, vs_s, vs_scales)

        pw = []
        for t in range(PACK):
            page = tile([P, C], F32, "pw%d" % t)
            nc.vector.memset(page[:], 0.0)
            pw.append(page)

        xo_gw = gather(xo_w, l2, U16, "xo_gw")
        xo_gs = gather(xo_s, l2, U8, "xo_gs")
        w2_d = deal_words(w2_w, U32, "w2_d", "p m t")
        w2_sd = deal_scales(w2_st, "w2_sd", 0)
        w0_d = deal_words(w0_w, U32, "w0_d", "p m t")
        w0_sd = deal_scales(w0_st, "w0_sd", 1)
        w_d = deal_words(w_w, U16, "w_d", "p t m")

        b_ps = [ps.tile([P, 2, J], F32, name="b_ps%d" % bank) for bank in range(2)]
        for t in range(PACK):
            cols = slice(t * P, (t + 1) * P)
            nc.tensor.matmul_mx(b_ps[t // 2][:, t % 2, :], lhsT=w2_d[:, cols].bitcast(E5M2), lhsT_scale=w2_sd[:, cols],
                                rhs=xo_gw[:].bitcast(E2M1), rhs_scale=xo_gs[:], start=True, stop=True)

        a_ps = [ps.tile([P, J], F32, name="a_ps%d" % t) for t in range(PACK)]
        for t in range(PACK):
            cols = slice(t * P, (t + 1) * P)
            nc.tensor.matmul_mx(a_ps[t][:], lhsT=w0_d[:, cols].bitcast(E5M2), lhsT_scale=w0_sd[:, cols],
                                rhs=xo_gw[:].bitcast(E2M1), rhs_scale=xo_gs[:], start=True, stop=False)

        b = []
        for t in range(PACK):
            rows = tile([P, J], F32, "b%d" % t)
            nc.scalar.activation(rows[:], b_ps[t // 2][:, t % 2, :], COPY)
            b.append(rows)

        xt_gw = gather(xt_w, l1, U32, "xt_gw")
        w_sd = deal_scales(w_st, "w_sd", 0)
        xt_gs = gather(xt_s, l1, U8, "xt_gs")
        for t in range(PACK):
            cols = slice(t * P, (t + 1) * P)
            nc.tensor.matmul_mx(a_ps[t][:], lhsT=w_d[:, cols].bitcast(E2M1), lhsT_scale=w_sd[:, cols],
                                rhs=xt_gw[:].bitcast(E4M3), rhs_scale=xt_gs[:], start=False, stop=True)

        a = [tile([P, J], F32, "a0")]
        nc.vector.tensor_copy(a[0][:], a_ps[0][:])
        for t in range(1, PACK):
            rows = tile([P, J], F32, "a%d" % t)
            nc.scalar.copy(rows[:], a_ps[t][:])
            a.append(rows)

        look4 = tile([P, PACK, O], F32, "look4")
        look5 = tile([P, PACK, O], F32, "look5")
        look6 = tile([P, PACK, O], F32, "look6")

        def board_at(t, lo, hi):
            return pw[t][:].indirect(l3[:, lo // PER_COLUMN : hi // PER_COLUMN])

        def look_b(t):
            nc.scalar.activation(look6[:, t, :], b[t][:].indirect(l6[:]), COPY, scale=a[t][:, 0:1])

        nc.vector.tensor_copy(board_at(0, 0, J), a[0][:])
        nc.scalar.activation(board_at(1, 0, J), a[1][:], COPY)
        nc.scalar.activation(board_at(3, 0, SCALAR_SHARE), a[3][:, 0:SCALAR_SHARE], COPY)
        nc.vector.tensor_copy(board_at(2, 0, J), a[2][:])
        nc.vector.tensor_copy(board_at(3, SCALAR_SHARE, J), a[3][:, SCALAR_SHARE:J])
        vs_gw = gather(vs_w, l7, U32, "vs_gw")
        vs_gs = gather(vs_s, l7, U8, "vs_gs")
        top = tile([P, PACK, O], F32, "top", shared_tag)

        for t in range(PACK // 2):
            look_b(t)
        for t in range(PACK):
            nc.scalar.activation(look4[:, t, :], pw[t][:].indirect(l4[:]), COPY, scale=b[t][:, 0:1])
            nc.scalar.activation(look5[:, t, :], pw[t][:].indirect(l5[:]), COPY, scale=b[t][:, LB2_SLOT : LB2_SLOT + 1])
            nc.vector.tensor_tensor(top[:, t, :], look4[:, t, :], look5[:, t, :], MAX)
        for t in range(PACK // 2, PACK):
            look_b(t)

        hid_b = tile([P, O, PACK], BF16, "hid_b")
        nc.vector.tensor_tensor(hid_b[:].rearrange("p (c i) t -> p c t i", i=4), top[:].rearrange("p t (c i) -> p c t i", i=4),
                                look6[:].rearrange("p t (c i) -> p c t i", i=4), SUB)
        hid_w = tile([P, O], U32, "hid_w")
        hid_s = tile([P, O], U8, "hid_s")
        nc.vector.quantize_mx(out=hid_w[:].bitcast(E4M3), scales=hid_s[:], in_=hid_b[:].rearrange("p o t -> p (o t)"))

        y = tile([P, 2, O], F32, "y")
        for h, (copy_out, queue) in enumerate(((nc.vector.tensor_copy, nc.sync), (nc.scalar.copy, nc.scalar))):
            cols = slice(h * P, (h + 1) * P)
            y_ps = ps.tile([P, O], F32, name="y_ps%d" % h)
            nc.tensor.matmul_mx(y_ps[:], lhsT=vs_gw[:, cols].bitcast(E5M2), lhsT_scale=vs_gs[:, cols],
                                rhs=hid_w[:].bitcast(E4M3), rhs_scale=hid_s[:], start=True, stop=True)
            copy_out(y[:, h, :], y_ps[:])
            queue.dma_start(out[cols, :], y[:, h, :])
